import numpy as np
import ml_dtypes


def mxq(x, axis, fmt="e4m3"):
    dtype, down = {"e4m3": (ml_dtypes.float8_e4m3fn, 7), "e5m2": (ml_dtypes.float8_e5m2, 14)}[fmt]
    v = np.moveaxis(np.asarray(x, np.float32).astype(ml_dtypes.bfloat16).astype(np.float64), axis, -1)
    blocks = v.reshape(v.shape[:-1] + (-1, 32))
    amax = np.abs(blocks).max(-1, keepdims=True)
    byte = np.maximum(np.where(amax > 0, np.frexp(amax)[1] - 1 + 127, 0) - down, 1)
    scale = np.exp2(byte - 127.0)
    codes = (blocks / scale).astype(np.float32).astype(dtype).astype(np.float64)
    return np.moveaxis((codes * scale).reshape(v.shape), -1, axis)


WIDE = False


def mx_kscale(k, group=512):
    if not WIDE:
        return np.ones(k)
    levels = np.array([18, -18])
    if group != 512:
        return np.exp2(np.random.permutation(np.resize(levels, k // group))).repeat(group)
    if k % 512:
        return np.exp2(np.random.permutation(np.resize(levels, k // 32))).repeat(32)
    a = np.empty((k // 512, 16))
    for p in range(k // 512):
        a[p, :8] = np.random.permutation(np.resize(levels, 8))
        for g in range(8):
            far = levels[np.abs(levels - a[p, g]) >= 10]
            a[p, g + 8] = far[np.random.randint(len(far))]
    return np.exp2(a.ravel()).repeat(32)


def f64(x):
    return np.asarray(x).astype(np.float64)


G, D, M, N = 4, 128, 256, 512


def setup_inputs():
    n = np.random.standard_normal
    s_d = mx_kscale(D, 0)
    return {
        "x": (n((G, D, M)) / s_d[:, None] / np.sqrt(D)).astype(np.float32),
        "c": (n((G, D, N)) * s_d[:, None] / np.sqrt(D)).astype(np.float32),
        "xn": (np.random.uniform(0.9, 1.3, (G, M, 1))).astype(np.float32),
        "cn": (np.random.uniform(0.9, 1.3, (G, 1, N))).astype(np.float32),
    }


def reference(x, c, xn, cn):
    xq = mxq(f64(x), 1, "e4m3")
    cq = mxq(f64(c), 1, "e4m3")
    z = xq.transpose(0, 2, 1) @ cq
    d2 = f64(xn) + f64(cn) - 2.0 * z
    r = 1.7320508 * np.sqrt(d2)
    y = (1.0 + r) * np.exp(-r)
    return y

@@ -1,0 +1,143 @@
+from contextlib import ExitStack
+
+import concourse.mybir as mybir
+
+G, D, M, N = 4, 128, 256, 512
+FLOPS = 2 * G * D * M * N
+
+F32 = mybir.dt.float32
+BF16 = mybir.dt.bfloat16
+U32 = mybir.dt.uint32
+U8 = mybir.dt.uint8
+FP8X4 = mybir.dt.float8_e4m3fn_x4
+ALU = mybir.AluOpType
+ACT = mybir.ActivationFunctionType
+
+P = 128
+PACK = 4
+ROWS = D // PACK
+CHUNK = 128
+HALF = N // 2
+TILES = M // P
+ROOT3_SQ = 1.7320508 * 1.7320508
+
+
+def tile_rows_kern_matern_kernel(tc, x, c, xn, cn, out):
+    nc = tc.nc
+    with ExitStack() as ctx:
+        sb = ctx.enter_context(tc.tile_pool(name="sb", bufs=1))
+        ps = ctx.enter_context(tc.psum_pool(name="ps", bufs=1))
+        ctx.enter_context(tc.manual_schedule())
+
+        x_rows = x.rearrange("g (p j) m -> (g p) j m", j=PACK)
+        c_rows = c.rearrange("g (p j) n -> (g p) j n", j=PACK)
+
+        x_raw = sb.tile([P, PACK, M], F32, name="x_raw")
+        nc.sync.dma_start(out=x_raw[:], in_=x_rows)
+
+        xn_rows = sb.tile([P, G * TILES * 32], F32, name="xn_rows", align_bytes=64)
+        nc.vector.memset(xn_rows[:], 0.0)
+        nc.sync.dma_start(
+            out=xn_rows[0:P:32, :].rearrange("q (b i) -> q b i", i=32),
+            in_=xn.rearrange("g (t q i) o -> q (g t) (i o)", q=4, i=32),
+        )
+
+        c_raw = []
+        cn_all = []
+        for h in range(2):
+            cols = slice(h * HALF, (h + 1) * HALF)
+            raw = sb.tile([P, PACK, HALF], F32, name="c_raw%d" % h)
+            nc.sync.dma_start(out=raw[:], in_=c_rows[:, :, cols])
+            c_raw.append(raw)
+            pairs = []
+            for gp in range(2):
+                spread = sb.tile([P, 2, HALF], F32, name="cn%d_%d" % (h, gp))
+                nc.sync.dma_start(out=spread[:], in_=cn[2 * gp : 2 * gp + 2, 0, cols].partition_broadcast(P))
+                pairs.append(spread)
+            cn_all.append(pairs)
+
+        def interleave(copy, raw, k, name):
+            grouped = sb.tile([P, CHUNK, PACK], BF16, name=name, align_bytes=64)
+            copy(
+                out=grouped[:].rearrange("p (c i) j -> p c j i", i=4),
+                in_=raw[:, :, k * CHUNK : (k + 1) * CHUNK].rearrange("p j (c i) -> p c j i", i=4),
+            )
+            return grouped
+
+        def quantize(grouped, name):
+            codes = sb.tile([P, CHUNK], U32, name=name + "_codes", align_bytes=64)
+            scales = sb.tile([P, CHUNK], U8, name=name + "_scales", align_bytes=64)
+            nc.vector.quantize_mx(
+                out=codes[:].bitcast(FP8X4), scales=scales[:], in_=grouped[:].rearrange("p c j -> p (c j)")
+            )
+            return codes, scales
+
+        xn_cols = sb.tile([P, G * TILES * 32], F32, name="xn_cols", align_bytes=64)
+        nc.vector.transpose(out=xn_cols[:], in_=xn_rows[:])
+        x_grp = [interleave(nc.vector.tensor_copy, x_raw, t, "x_grp%d" % t) for t in range(TILES)]
+        bias = sb.tile([P, G * TILES], F32, name="bias")
+        nc.vector.tensor_scalar(
+            out=bias[:], in0=xn_cols[:, 0 : G * TILES * 32 : 32], scalar1=ROOT3_SQ, scalar2=None, op0=ALU.mult
+        )
+        xq = [quantize(x_grp[t], "xq%d" % t) for t in range(TILES)]
+
+        banks = [[ps.tile([P, TILES, HALF], F32, name="z%d_%d" % (g, h)) for h in range(2)] for g in range(G)]
+        r = [[sb.tile([P, N], F32, name="r%d_%d" % (g, t)) for t in range(TILES)] for g in range(G)]
+
+        def products(h, cq):
+            for g in range(G):
+                rows = slice(ROWS * g, ROWS * (g + 1))
+                for k in range(2):
+                    for t in range(TILES):
+                        nc.tensor.matmul_mx(
+                            out=banks[g][h][:, t, k * CHUNK : (k + 1) * CHUNK],
+                            lhsT=xq[t][0][rows, :].bitcast(FP8X4),
+                            lhsT_scale=xq[t][1][rows, :],
+                            rhs=cq[k][0][rows, :].bitcast(FP8X4),
+                            rhs_scale=cq[k][1][rows, :],
+                            start=True,
+                            stop=True,
+                        )
+
+        def roots(g, h):
+            part = sb.tile([P, TILES, HALF], F32, name="part%d_%d" % (g, h))
+            nc.vector.scalar_tensor_tensor(
+                out=part[:],
+                in0=banks[g][h][:],
+                scalar=-2.0,
+                in1=cn_all[h][g // 2][:, g % 2, :].unsqueeze(1).to_broadcast([P, TILES, HALF]),
+                op0=ALU.mult,
+                op1=ALU.add,
+            )
+            for t in range(TILES):
+                nc.scalar.activation(
+                    out=r[g][t][:, h * HALF : (h + 1) * HALF],
+                    in_=part[:, t, :],
+                    func=ACT.Sqrt,
+                    bias=bias[:, TILES * g + t : TILES * g + t + 1],
+                    scale=ROOT3_SQ,
+                )
+
+        c_grp0 = [interleave(nc.vector.tensor_copy, c_raw[0], k, "c_grp0_%d" % k) for k in range(2)]
+        products(0, [quantize(c_grp0[k], "cq0_%d" % k) for k in range(2)])
+        roots(0, 0)
+        roots(1, 0)
+        c_grp1 = [
+            interleave(nc.vector.tensor_copy, c_raw[1], 0, "c_grp1_0"),
+            interleave(nc.scalar.copy, c_raw[1], 1, "c_grp1_1"),
+        ]
+        roots(2, 0)
+        products(1, [quantize(c_grp1[k], "cq1_%d" % k) for k in range(2)])
+        roots(3, 0)
+        for g in range(G):
+            roots(g, 1)
+
+        for g in range(G):
+            for t in range(TILES):
+                decay = sb.tile([P, N], F32, name="decay%d_%d" % (g, t))
+                nc.scalar.activation(out=decay[:], in_=r[g][t][:], func=ACT.Exp, scale=-1.0)
+                y = sb.tile([P, N], F32, name="y%d_%d" % (g, t))
+                nc.vector.scalar_tensor_tensor(
+                    out=y[:], in0=r[g][t][:], scalar=1.0, in1=decay[:], op0=ALU.add, op1=ALU.mult
+                )
+                nc.sync.dma_start(out=out[g, t * P : (t + 1) * P, :], in_=y[:])

@@ -32,29 +32,27 @@ def tile_rows_kern_matern_kernel(tc, x, c, xn, cn, out):
         x_rows = x.rearrange("g (p j) m -> (g p) j m", j=PACK)
         c_rows = c.rearrange("g (p j) n -> (g p) j n", j=PACK)
 
+        ones = sb.tile([P, 1], F32, name="ones")
+        nc.vector.memset(ones[:], 1.0)
+        one = sb.tile([P, 1], F32, name="one")
+        nc.scalar.activation(out=one[:], in_=ones[:], func=ACT.Sqrt)
+
+        cn_rows = sb.tile([P, 32], F32, name="cn_rows", align_bytes=64)
+        nc.sync.dma_start(
+            out=cn_rows[:], in_=cn[0:2, 0, :].rearrange("g (b j) -> (g b) j", j=32).partition_broadcast(4)
+        )
         x_raw = sb.tile([P, PACK, M], F32, name="x_raw")
         nc.sync.dma_start(out=x_raw[:], in_=x_rows)
-
-        xn_rows = sb.tile([P, G * TILES * 32], F32, name="xn_rows", align_bytes=64)
+        xn_rows = sb.tile([P, 32], F32, name="xn_rows", align_bytes=64)
         nc.vector.memset(xn_rows[:], 0.0)
-        nc.sync.dma_start(
-            out=xn_rows[0:P:32, :].rearrange("q (b i) -> q b i", i=32),
-            in_=xn.rearrange("g (t q i) o -> q (g t) (i o)", q=4, i=32),
-        )
-
+        nc.sync.dma_start(out=xn_rows[0:P:4, :], in_=xn.rearrange("g (t q i) o -> q (g t) (i o)", q=4, i=32))
         c_raw = []
-        cn_all = []
         for h in range(2):
-            cols = slice(h * HALF, (h + 1) * HALF)
             raw = sb.tile([P, PACK, HALF], F32, name="c_raw%d" % h)
-            nc.sync.dma_start(out=raw[:], in_=c_rows[:, :, cols])
+            nc.sync.dma_start(out=raw[:], in_=c_rows[:, :, h * HALF : (h + 1) * HALF])
             c_raw.append(raw)
-            pairs = []
-            for gp in range(2):
-                spread = sb.tile([P, 2, HALF], F32, name="cn%d_%d" % (h, gp))
-                nc.sync.dma_start(out=spread[:], in_=cn[2 * gp : 2 * gp + 2, 0, cols].partition_broadcast(P))
-                pairs.append(spread)
-            cn_all.append(pairs)
+        cn_late = sb.tile([P, 2, N], F32, name="cn_late")
+        nc.sync.dma_start(out=cn_late[:], in_=cn[2:4, 0, :].partition_broadcast(P))
 
         def interleave(copy, raw, k, name):
             grouped = sb.tile([P, CHUNK, PACK], BF16, name=name, align_bytes=64)
@@ -72,23 +70,32 @@ def tile_rows_kern_matern_kernel(tc, x, c, xn, cn, out):
             )
             return codes, scales
 
-        xn_cols = sb.tile([P, G * TILES * 32], F32, name="xn_cols", align_bytes=64)
-        nc.vector.transpose(out=xn_cols[:], in_=xn_rows[:])
-        x_grp = [interleave(nc.vector.tensor_copy, x_raw, t, "x_grp%d" % t) for t in range(TILES)]
+        cn_cols = sb.tile([P, 32], F32, name="cn_cols", align_bytes=64)
+        nc.vector.transpose(out=cn_cols[:], in_=cn_rows[:])
+        xn_cols = sb.tile([P, 32], F32, name="xn_cols", align_bytes=64)
         bias = sb.tile([P, G * TILES], F32, name="bias")
-        nc.vector.tensor_scalar(
-            out=bias[:], in0=xn_cols[:, 0 : G * TILES * 32 : 32], scalar1=ROOT3_SQ, scalar2=None, op0=ALU.mult
-        )
-        xq = [quantize(x_grp[t], "xq%d" % t) for t in range(TILES)]
+
+        def repeat_cn(h):
+            wide = sb.tile([P, 2, 8, 32], F32, name="cn_wide%d" % h, align_bytes=64)
+            blocks = cn_cols[:].rearrange("p (g h w) -> p g h w", g=2, h=2)[:, :, h, :]
+            nc.scalar.copy(out=wide[:], in_=blocks.unsqueeze(3).to_broadcast([P, 2, 8, 32]))
+            return wide
+
+        def spread_cn(wide, h):
+            spread = sb.tile([P, 2, HALF], F32, name="cn_early%d" % h, align_bytes=64)
+            nc.vector.transpose(
+                out=spread[:].rearrange("p g n -> p (g n)"), in_=wide[:].rearrange("p g w i -> p (g w i)")
+            )
+            return spread
 
         banks = [[ps.tile([P, TILES, HALF], F32, name="z%d_%d" % (g, h)) for h in range(2)] for g in range(G)]
         r = [[sb.tile([P, N], F32, name="r%d_%d" % (g, t)) for t in range(TILES)] for g in range(G)]
 
-        def products(h, cq):
-            for g in range(G):
-                rows = slice(ROWS * g, ROWS * (g + 1))
-                for k in range(2):
-                    for t in range(TILES):
+        def products(h, pair, xq, cq):
+            for k in range(2):
+                for t in range(TILES):
+                    for g in (2 * pair, 2 * pair + 1):
+                        rows = slice(ROWS * g, ROWS * (g + 1))
                         nc.tensor.matmul_mx(
                             out=banks[g][h][:, t, k * CHUNK : (k + 1) * CHUNK],
                             lhsT=xq[t][0][rows, :].bitcast(FP8X4),
@@ -99,13 +106,13 @@ def tile_rows_kern_matern_kernel(tc, x, c, xn, cn, out):
                             stop=True,
                         )
 
-        def roots(g, h):
+        def roots(g, h, cn_row):
             part = sb.tile([P, TILES, HALF], F32, name="part%d_%d" % (g, h))
             nc.vector.scalar_tensor_tensor(
                 out=part[:],
                 in0=banks[g][h][:],
                 scalar=-2.0,
-                in1=cn_all[h][g // 2][:, g % 2, :].unsqueeze(1).to_broadcast([P, TILES, HALF]),
+                in1=cn_row.unsqueeze(1).to_broadcast([P, TILES, HALF]),
                 op0=ALU.mult,
                 op1=ALU.add,
             )
@@ -118,26 +125,46 @@ def tile_rows_kern_matern_kernel(tc, x, c, xn, cn, out):
                     scale=ROOT3_SQ,
                 )
 
-        c_grp0 = [interleave(nc.vector.tensor_copy, c_raw[0], k, "c_grp0_%d" % k) for k in range(2)]
-        products(0, [quantize(c_grp0[k], "cq0_%d" % k) for k in range(2)])
-        roots(0, 0)
-        roots(1, 0)
+        wide0 = repeat_cn(0)
+        cn_early = [spread_cn(wide0, 0)]
+        x_grp = [
+            interleave(nc.vector.tensor_copy, x_raw, 0, "x_grp0"),
+            interleave(nc.scalar.copy, x_raw, 1, "x_grp1"),
+        ]
+        nc.vector.transpose(out=xn_cols[:], in_=xn_rows[:])
+        wide1 = repeat_cn(1)
+        xq = [quantize(x_grp[t], "xq%d" % t) for t in range(TILES)]
+        nc.vector.tensor_scalar(out=bias[:], in0=xn_cols[:, 0:32:4], scalar1=ROOT3_SQ, scalar2=None, op0=ALU.mult)
+        c_grp0 = [
+            interleave(nc.vector.tensor_copy, c_raw[0], 0, "c_grp0_0"),
+            interleave(nc.scalar.copy, c_raw[0], 1, "c_grp0_1"),
+        ]
+        cn_early.append(spread_cn(wide1, 1))
+        cq0 = [quantize(c_grp0[k], "cq0_%d" % k) for k in range(2)]
+        products(0, 0, xq, cq0)
+        products(0, 1, xq, cq0)
         c_grp1 = [
             interleave(nc.vector.tensor_copy, c_raw[1], 0, "c_grp1_0"),
             interleave(nc.scalar.copy, c_raw[1], 1, "c_grp1_1"),
         ]
-        roots(2, 0)
-        products(1, [quantize(c_grp1[k], "cq1_%d" % k) for k in range(2)])
-        roots(3, 0)
-        for g in range(G):
-            roots(g, 1)
+        roots(0, 0, cn_early[0][:, 0, :])
+        cq1 = [quantize(c_grp1[k], "cq1_%d" % k) for k in range(2)]
+        products(1, 0, xq, cq1)
+        products(1, 1, xq, cq1)
+        roots(1, 0, cn_early[0][:, 1, :])
+        for g in range(2):
+            roots(g, 1, cn_early[1][:, g, :])
+        for h in range(2):
+            for g in range(2, G):
+                roots(g, h, cn_late[:, g - 2, h * HALF : (h + 1) * HALF])
 
-        for g in range(G):
-            for t in range(TILES):
-                decay = sb.tile([P, N], F32, name="decay%d_%d" % (g, t))
-                nc.scalar.activation(out=decay[:], in_=r[g][t][:], func=ACT.Exp, scale=-1.0)
-                y = sb.tile([P, N], F32, name="y%d_%d" % (g, t))
-                nc.vector.scalar_tensor_tensor(
-                    out=y[:], in0=r[g][t][:], scalar=1.0, in1=decay[:], op0=ALU.add, op1=ALU.mult
-                )
-                nc.sync.dma_start(out=out[g, t * P : (t + 1) * P, :], in_=y[:])
+        pieces = [(g, t, 0, N) for g in range(G) for t in range(TILES)]
+        pieces = [(0, 0, 0, HALF), (0, 0, HALF, N)] + pieces[1:-1] + [(G - 1, 1, 0, HALF), (G - 1, 1, HALF, N)]
+        for g, t, n0, n1 in pieces:
+            decay = sb.tile([P, n1 - n0], F32, name="decay%d_%d_%d" % (g, t, n0))
+            nc.scalar.activation(out=decay[:], in_=r[g][t][:, n0:n1], func=ACT.Exp, scale=-1.0)
+            y = sb.tile([P, n1 - n0], F32, name="y%d_%d_%d" % (g, t, n0))
+            nc.vector.scalar_tensor_tensor(
+                out=y[:], in0=r[g][t][:, n0:n1], scalar=one[:], in1=decay[:], op0=ALU.add, op1=ALU.mult
+            )
+            nc.sync.dma_start(out=out[g, t * P : (t + 1) * P, n0:n1], in_=y[:])

@@ -32,27 +32,29 @@ def tile_rows_kern_matern_kernel(tc, x, c, xn, cn, out):
         x_rows = x.rearrange("g (p j) m -> (g p) j m", j=PACK)
         c_rows = c.rearrange("g (p j) n -> (g p) j n", j=PACK)
 
+        cn_rows = sb.tile([P, 32], F32, name="cn_rows", align_bytes=64)
+        for q in range(4):
+            nc.scalar.dma_start(
+                out=cn_rows[32 * q : 32 * (q + 1), :], in_=cn[0:2, 0, :].rearrange("g (b j) -> (g b) j", j=32)
+            )
         ones = sb.tile([P, 1], F32, name="ones")
         nc.vector.memset(ones[:], 1.0)
         one = sb.tile([P, 1], F32, name="one")
         nc.scalar.activation(out=one[:], in_=ones[:], func=ACT.Sqrt)
 
-        cn_rows = sb.tile([P, 32], F32, name="cn_rows", align_bytes=64)
-        nc.sync.dma_start(
-            out=cn_rows[:], in_=cn[0:2, 0, :].rearrange("g (b j) -> (g b) j", j=32).partition_broadcast(4)
-        )
         x_raw = sb.tile([P, PACK, M], F32, name="x_raw")
         nc.sync.dma_start(out=x_raw[:], in_=x_rows)
+        c_raw = [sb.tile([P, PACK, HALF], F32, name="c_raw%d" % h) for h in range(2)]
+        nc.sync.dma_start(out=c_raw[0][:], in_=c_rows[:, :, 0:HALF])
         xn_rows = sb.tile([P, 32], F32, name="xn_rows", align_bytes=64)
         nc.vector.memset(xn_rows[:], 0.0)
         nc.sync.dma_start(out=xn_rows[0:P:4, :], in_=xn.rearrange("g (t q i) o -> q (g t) (i o)", q=4, i=32))
-        c_raw = []
-        for h in range(2):
-            raw = sb.tile([P, PACK, HALF], F32, name="c_raw%d" % h)
-            nc.sync.dma_start(out=raw[:], in_=c_rows[:, :, h * HALF : (h + 1) * HALF])
-            c_raw.append(raw)
-        cn_late = sb.tile([P, 2, N], F32, name="cn_late")
-        nc.sync.dma_start(out=cn_late[:], in_=cn[2:4, 0, :].partition_broadcast(P))
+        nc.sync.dma_start(out=c_raw[1][:], in_=c_rows[:, :, HALF:N])
+        cn_late = []
+        for g in range(2, G):
+            spread = sb.tile([P, N], F32, name="cn_late%d" % g)
+            nc.sync.dma_start(out=spread[:], in_=cn[g, 0, :].partition_broadcast(P))
+            cn_late.append(spread)
 
         def interleave(copy, raw, k, name):
             grouped = sb.tile([P, CHUNK, PACK], BF16, name=name, align_bytes=64)
@@ -106,60 +108,59 @@ def tile_rows_kern_matern_kernel(tc, x, c, xn, cn, out):
                             stop=True,
                         )
 
-        def roots(g, h, cn_row):
-            part = sb.tile([P, TILES, HALF], F32, name="part%d_%d" % (g, h))
+        def roots(g, h, cn_row, t0=0, t1=TILES):
+            part = sb.tile([P, t1 - t0, HALF], F32, name="part%d_%d_%d" % (g, h, t0))
             nc.vector.scalar_tensor_tensor(
                 out=part[:],
-                in0=banks[g][h][:],
+                in0=banks[g][h][:, t0:t1, :],
                 scalar=-2.0,
-                in1=cn_row.unsqueeze(1).to_broadcast([P, TILES, HALF]),
+                in1=cn_row.unsqueeze(1).to_broadcast([P, t1 - t0, HALF]),
                 op0=ALU.mult,
                 op1=ALU.add,
             )
-            for t in range(TILES):
+            for t in range(t0, t1):
                 nc.scalar.activation(
                     out=r[g][t][:, h * HALF : (h + 1) * HALF],
-                    in_=part[:, t, :],
+                    in_=part[:, t - t0, :],
                     func=ACT.Sqrt,
                     bias=bias[:, TILES * g + t : TILES * g + t + 1],
                     scale=ROOT3_SQ,
                 )
 
         wide0 = repeat_cn(0)
+        wide1 = repeat_cn(1)
         cn_early = [spread_cn(wide0, 0)]
         x_grp = [
             interleave(nc.vector.tensor_copy, x_raw, 0, "x_grp0"),
             interleave(nc.scalar.copy, x_raw, 1, "x_grp1"),
         ]
-        nc.vector.transpose(out=xn_cols[:], in_=xn_rows[:])
-        wide1 = repeat_cn(1)
         xq = [quantize(x_grp[t], "xq%d" % t) for t in range(TILES)]
-        nc.vector.tensor_scalar(out=bias[:], in0=xn_cols[:, 0:32:4], scalar1=ROOT3_SQ, scalar2=None, op0=ALU.mult)
         c_grp0 = [
             interleave(nc.vector.tensor_copy, c_raw[0], 0, "c_grp0_0"),
             interleave(nc.scalar.copy, c_raw[0], 1, "c_grp0_1"),
         ]
-        cn_early.append(spread_cn(wide1, 1))
+        nc.vector.transpose(out=xn_cols[:], in_=xn_rows[:])
         cq0 = [quantize(c_grp0[k], "cq0_%d" % k) for k in range(2)]
         products(0, 0, xq, cq0)
-        products(0, 1, xq, cq0)
-        c_grp1 = [
-            interleave(nc.vector.tensor_copy, c_raw[1], 0, "c_grp1_0"),
-            interleave(nc.scalar.copy, c_raw[1], 1, "c_grp1_1"),
-        ]
+        nc.vector.tensor_scalar(out=bias[:], in0=xn_cols[:, 0:32:4], scalar1=ROOT3_SQ, scalar2=None, op0=ALU.mult)
+        cn_early.append(spread_cn(wide1, 1))
+        c_grp1 = [interleave(nc.scalar.copy, c_raw[1], k, "c_grp1_%d" % k) for k in range(2)]
         roots(0, 0, cn_early[0][:, 0, :])
         cq1 = [quantize(c_grp1[k], "cq1_%d" % k) for k in range(2)]
         products(1, 0, xq, cq1)
+        products(0, 1, xq, cq0)
         products(1, 1, xq, cq1)
         roots(1, 0, cn_early[0][:, 1, :])
         for g in range(2):
             roots(g, 1, cn_early[1][:, g, :])
-        for h in range(2):
-            for g in range(2, G):
-                roots(g, h, cn_late[:, g - 2, h * HALF : (h + 1) * HALF])
+        roots(2, 0, cn_late[0][:, 0:HALF])
+        roots(2, 1, cn_late[0][:, HALF:N])
+        roots(3, 0, cn_late[1][:, 0:HALF])
+        for t in range(TILES):
+            roots(3, 1, cn_late[1][:, HALF:N], t, t + 1)
 
         pieces = [(g, t, 0, N) for g in range(G) for t in range(TILES)]
-        pieces = [(0, 0, 0, HALF), (0, 0, HALF, N)] + pieces[1:-1] + [(G - 1, 1, 0, HALF), (G - 1, 1, HALF, N)]
+        pieces = [(0, 0, 0, HALF), (0, 0, HALF, N)] + pieces[1:-1] + [(G - 1, 1, 0, HALF), (G - 1, 1, HALF, 384), (G - 1, 1, 384, N)]
         for g, t, n0, n1 in pieces:
             decay = sb.tile([P, n1 - n0], F32, name="decay%d_%d_%d" % (g, t, n0))
             nc.scalar.activation(out=decay[:], in_=r[g][t][:, n0:n1], func=ACT.Exp, scale=-1.0)

@@ -32,16 +32,15 @@ def tile_rows_kern_matern_kernel(tc, x, c, xn, cn, out):
         x_rows = x.rearrange("g (p j) m -> (g p) j m", j=PACK)
         c_rows = c.rearrange("g (p j) n -> (g p) j n", j=PACK)
 
-        cn_rows = sb.tile([P, 32], F32, name="cn_rows", align_bytes=64)
-        for q in range(4):
-            nc.scalar.dma_start(
-                out=cn_rows[32 * q : 32 * (q + 1), :], in_=cn[0:2, 0, :].rearrange("g (b j) -> (g b) j", j=32)
-            )
         ones = sb.tile([P, 1], F32, name="ones")
         nc.vector.memset(ones[:], 1.0)
         one = sb.tile([P, 1], F32, name="one")
         nc.scalar.activation(out=one[:], in_=ones[:], func=ACT.Sqrt)
 
+        cn_rows = sb.tile([P, 32], F32, name="cn_rows", align_bytes=64)
+        nc.sync.dma_start(
+            out=cn_rows[:], in_=cn[0:2, 0, :].rearrange("g (b j) -> (g b) j", j=32).partition_broadcast(4)
+        )
         x_raw = sb.tile([P, PACK, M], F32, name="x_raw")
         nc.sync.dma_start(out=x_raw[:], in_=x_rows)
         c_raw = [sb.tile([P, PACK, HALF], F32, name="c_raw%d" % h) for h in range(2)]
@@ -56,31 +55,40 @@ def tile_rows_kern_matern_kernel(tc, x, c, xn, cn, out):
             nc.sync.dma_start(out=spread[:], in_=cn[g, 0, :].partition_broadcast(P))
             cn_late.append(spread)
 
-        def interleave(copy, raw, k, name):
-            grouped = sb.tile([P, CHUNK, PACK], BF16, name=name, align_bytes=64)
+        def interleave(copy, grouped, raw, k):
+            cols = slice(k * CHUNK, (k + 1) * CHUNK)
             copy(
-                out=grouped[:].rearrange("p (c i) j -> p c j i", i=4),
-                in_=raw[:, :, k * CHUNK : (k + 1) * CHUNK].rearrange("p j (c i) -> p c j i", i=4),
+                out=grouped[:, cols, :].rearrange("p (c i) j -> p c j i", i=4),
+                in_=raw[:, :, cols].rearrange("p j (c i) -> p c j i", i=4),
             )
-            return grouped
 
-        def quantize(grouped, name):
-            codes = sb.tile([P, CHUNK], U32, name=name + "_codes", align_bytes=64)
-            scales = sb.tile([P, CHUNK], U8, name=name + "_scales", align_bytes=64)
+        def operand(name):
+            grouped = sb.tile([P, 2 * CHUNK, PACK], BF16, name=name + "_grouped", align_bytes=64)
+            codes = sb.tile([P, 2 * CHUNK], U32, name=name + "_codes", align_bytes=64)
+            scales = sb.tile([P, 2 * CHUNK], U8, name=name + "_scales", align_bytes=64)
+            return grouped, codes, scales
+
+        def quantize(op, k0, k1):
+            grouped, codes, scales = op
+            cols = slice(k0 * CHUNK, k1 * CHUNK)
             nc.vector.quantize_mx(
-                out=codes[:].bitcast(FP8X4), scales=scales[:], in_=grouped[:].rearrange("p c j -> p (c j)")
+                out=codes[:, cols].bitcast(FP8X4),
+                scales=scales[:, cols],
+                in_=grouped[:, cols, :].rearrange("p c j -> p (c j)"),
             )
-            return codes, scales
+
+        xq = operand("x")
+        cq = [operand("c%d" % h) for h in range(2)]
 
         cn_cols = sb.tile([P, 32], F32, name="cn_cols", align_bytes=64)
         nc.vector.transpose(out=cn_cols[:], in_=cn_rows[:])
         xn_cols = sb.tile([P, 32], F32, name="xn_cols", align_bytes=64)
         bias = sb.tile([P, G * TILES], F32, name="bias")
 
-        def repeat_cn(h):
+        def repeat_cn(copy, h):
             wide = sb.tile([P, 2, 8, 32], F32, name="cn_wide%d" % h, align_bytes=64)
             blocks = cn_cols[:].rearrange("p (g h w) -> p g h w", g=2, h=2)[:, :, h, :]
-            nc.scalar.copy(out=wide[:], in_=blocks.unsqueeze(3).to_broadcast([P, 2, 8, 32]))
+            copy(out=wide[:], in_=blocks.unsqueeze(3).to_broadcast([P, 2, 8, 32]))
             return wide
 
         def spread_cn(wide, h):
@@ -90,82 +98,114 @@ def tile_rows_kern_matern_kernel(tc, x, c, xn, cn, out):
             )
             return spread
 
-        banks = [[ps.tile([P, TILES, HALF], F32, name="z%d_%d" % (g, h)) for h in range(2)] for g in range(G)]
+        banks = [[ps.tile([P, N], F32, name="z%d_%d" % (g, b)) for b in range(2)] for g in range(G)]
         r = [[sb.tile([P, N], F32, name="r%d_%d" % (g, t)) for t in range(TILES)] for g in range(G)]
 
-        def products(h, pair, xq, cq):
+        def product(z, g, t, h, k):
+            rows = slice(ROWS * g, ROWS * (g + 1))
+            m_cols = slice(t * P, (t + 1) * P)
+            n_cols = slice(k * CHUNK, (k + 1) * CHUNK)
+            nc.tensor.matmul_mx(
+                out=z,
+                lhsT=xq[1][rows, m_cols].bitcast(FP8X4),
+                lhsT_scale=xq[2][rows, m_cols],
+                rhs=cq[h][1][rows, n_cols].bitcast(FP8X4),
+                rhs_scale=cq[h][2][rows, n_cols],
+                start=True,
+                stop=True,
+            )
+
+        def products_by_half(g, h):
             for k in range(2):
                 for t in range(TILES):
-                    for g in (2 * pair, 2 * pair + 1):
-                        rows = slice(ROWS * g, ROWS * (g + 1))
-                        nc.tensor.matmul_mx(
-                            out=banks[g][h][:, t, k * CHUNK : (k + 1) * CHUNK],
-                            lhsT=xq[t][0][rows, :].bitcast(FP8X4),
-                            lhsT_scale=xq[t][1][rows, :],
-                            rhs=cq[k][0][rows, :].bitcast(FP8X4),
-                            rhs_scale=cq[k][1][rows, :],
-                            start=True,
-                            stop=True,
-                        )
+                    c0 = t * HALF + k * CHUNK
+                    product(banks[g][h][:, c0 : c0 + CHUNK], g, t, h, k)
 
-        def roots(g, h, cn_row, t0=0, t1=TILES):
+        def products_by_tile(g, t):
+            for h in range(2):
+                for k in range(2):
+                    c0 = h * HALF + k * CHUNK
+                    product(banks[g][t][:, c0 : c0 + CHUNK], g, t, h, k)
+
+        def root(g, t, n0, n1, part):
+            nc.scalar.activation(
+                out=r[g][t][:, n0:n1],
+                in_=part,
+                func=ACT.Sqrt,
+                bias=bias[:, TILES * g + t : TILES * g + t + 1],
+                scale=ROOT3_SQ,
+            )
+
+        def roots_by_half(g, h, t0, t1):
             part = sb.tile([P, t1 - t0, HALF], F32, name="part%d_%d_%d" % (g, h, t0))
             nc.vector.scalar_tensor_tensor(
                 out=part[:],
-                in0=banks[g][h][:, t0:t1, :],
+                in0=banks[g][h][:].rearrange("p (t n) -> p t n", t=TILES)[:, t0:t1, :],
                 scalar=-2.0,
-                in1=cn_row.unsqueeze(1).to_broadcast([P, t1 - t0, HALF]),
+                in1=cn_early[h][:, g, :].unsqueeze(1).to_broadcast([P, t1 - t0, HALF]),
                 op0=ALU.mult,
                 op1=ALU.add,
             )
             for t in range(t0, t1):
-                nc.scalar.activation(
-                    out=r[g][t][:, h * HALF : (h + 1) * HALF],
-                    in_=part[:, t - t0, :],
-                    func=ACT.Sqrt,
-                    bias=bias[:, TILES * g + t : TILES * g + t + 1],
-                    scale=ROOT3_SQ,
-                )
+                root(g, t, h * HALF, (h + 1) * HALF, part[:, t - t0, :])
 
-        wide0 = repeat_cn(0)
-        wide1 = repeat_cn(1)
-        cn_early = [spread_cn(wide0, 0)]
-        x_grp = [
-            interleave(nc.vector.tensor_copy, x_raw, 0, "x_grp0"),
-            interleave(nc.scalar.copy, x_raw, 1, "x_grp1"),
-        ]
-        xq = [quantize(x_grp[t], "xq%d" % t) for t in range(TILES)]
-        c_grp0 = [
-            interleave(nc.vector.tensor_copy, c_raw[0], 0, "c_grp0_0"),
-            interleave(nc.scalar.copy, c_raw[0], 1, "c_grp0_1"),
-        ]
-        nc.vector.transpose(out=xn_cols[:], in_=xn_rows[:])
-        cq0 = [quantize(c_grp0[k], "cq0_%d" % k) for k in range(2)]
-        products(0, 0, xq, cq0)
-        nc.vector.tensor_scalar(out=bias[:], in0=xn_cols[:, 0:32:4], scalar1=ROOT3_SQ, scalar2=None, op0=ALU.mult)
-        cn_early.append(spread_cn(wide1, 1))
-        c_grp1 = [interleave(nc.scalar.copy, c_raw[1], k, "c_grp1_%d" % k) for k in range(2)]
-        roots(0, 0, cn_early[0][:, 0, :])
-        cq1 = [quantize(c_grp1[k], "cq1_%d" % k) for k in range(2)]
-        products(1, 0, xq, cq1)
-        products(0, 1, xq, cq0)
-        products(1, 1, xq, cq1)
-        roots(1, 0, cn_early[0][:, 1, :])
-        for g in range(2):
-            roots(g, 1, cn_early[1][:, g, :])
-        roots(2, 0, cn_late[0][:, 0:HALF])
-        roots(2, 1, cn_late[0][:, HALF:N])
-        roots(3, 0, cn_late[1][:, 0:HALF])
-        for t in range(TILES):
-            roots(3, 1, cn_late[1][:, HALF:N], t, t + 1)
-
-        pieces = [(g, t, 0, N) for g in range(G) for t in range(TILES)]
-        pieces = [(0, 0, 0, HALF), (0, 0, HALF, N)] + pieces[1:-1] + [(G - 1, 1, 0, HALF), (G - 1, 1, HALF, 384), (G - 1, 1, 384, N)]
-        for g, t, n0, n1 in pieces:
-            decay = sb.tile([P, n1 - n0], F32, name="decay%d_%d_%d" % (g, t, n0))
-            nc.scalar.activation(out=decay[:], in_=r[g][t][:, n0:n1], func=ACT.Exp, scale=-1.0)
-            y = sb.tile([P, n1 - n0], F32, name="y%d_%d_%d" % (g, t, n0))
+        def roots_by_tile(g, t, n0, n1):
+            part = sb.tile([P, n1 - n0], F32, name="part%d_%d_%d" % (g, t, n0))
             nc.vector.scalar_tensor_tensor(
-                out=y[:], in0=r[g][t][:, n0:n1], scalar=one[:], in1=decay[:], op0=ALU.add, op1=ALU.mult
+                out=part[:],
+                in0=banks[g][t][:, n0:n1],
+                scalar=-2.0,
+                in1=cn_late[g - 2][:, n0:n1],
+                op0=ALU.mult,
+                op1=ALU.add,
             )
-            nc.sync.dma_start(out=out[g, t * P : (t + 1) * P, n0:n1], in_=y[:])
+            root(g, t, n0, n1, part[:])
+
+        wide = [repeat_cn(nc.vector.tensor_copy, 0), repeat_cn(nc.scalar.copy, 1)]
+        cn_early = [spread_cn(wide[h], h) for h in range(2)]
+        for t in range(TILES):
+            interleave(nc.scalar.copy, xq[0], x_raw, t)
+        interleave(nc.vector.tensor_copy, cq[0][0], c_raw[0], 0)
+        interleave(nc.scalar.copy, cq[0][0], c_raw[0], 1)
+        nc.vector.transpose(out=xn_cols[:], in_=xn_rows[:])
+        quantize(xq, 0, 2)
+        quantize(cq[0], 0, 1)
+        quantize(cq[0], 1, 2)
+        for g in range(2):
+            products_by_half(g, 0)
+        interleave(nc.vector.tensor_copy, cq[1][0], c_raw[1], 0)
+        interleave(nc.scalar.copy, cq[1][0], c_raw[1], 1)
+        nc.vector.tensor_scalar(out=bias[:], in0=xn_cols[:, 0:32:4], scalar1=ROOT3_SQ, scalar2=None, op0=ALU.mult)
+        quantize(cq[1], 0, 2)
+        for g in range(2):
+            products_by_half(g, 1)
+        for g in range(2, G):
+            for t in range(TILES):
+                products_by_tile(g, t)
+        for t in range(TILES):
+            roots_by_half(0, 0, t, t + 1)
+        roots_by_half(1, 0, 0, TILES)
+        for g in range(2):
+            roots_by_half(g, 1, 0, TILES)
+        roots_by_tile(2, 0, 0, N)
+        roots_by_tile(2, 1, 0, N)
+        roots_by_tile(3, 0, 0, N)
+        roots_by_tile(3, 1, 0, HALF)
+        roots_by_tile(3, 1, HALF, N)
+
+        for g in range(G):
+            for t in range(TILES):
+                last = g == G - 1 and t == TILES - 1
+                edge = last or (g == 0 and t == 0)
+                cuts = (0, HALF, HALF + CHUNK, N) if last else (0, HALF, N)
+                y = sb.tile([P, N], F32, name="y%d_%d" % (g, t))
+                for n0, n1 in zip(cuts, cuts[1:]):
+                    decay = sb.tile([P, n1 - n0], F32, name="decay%d_%d_%d" % (g, t, n0))
+                    nc.scalar.activation(out=decay[:], in_=r[g][t][:, n0:n1], func=ACT.Exp, scale=-1.0)
+                    nc.vector.scalar_tensor_tensor(
+                        out=y[:, n0:n1], in0=r[g][t][:, n0:n1], scalar=one[:], in1=decay[:], op0=ALU.add, op1=ALU.mult
+                    )
+                    if edge:
+                        nc.sync.dma_start(out=out[g, t * P : (t + 1) * P, n0:n1], in_=y[:, n0:n1])
+                if not edge:
+                    nc.sync.dma_start(out=out[g, t * P : (t + 1) * P, :], in_=y[:])

@@ -50,9 +50,9 @@ def tile_rows_kern_matern_kernel(tc, x, c, xn, cn, out):
         nc.sync.dma_start(out=xn_rows[0:P:4, :], in_=xn.rearrange("g (t q i) o -> q (g t) (i o)", q=4, i=32))
         nc.sync.dma_start(out=c_raw[1][:], in_=c_rows[:, :, HALF:N])
         cn_late = []
-        for g in range(2, G):
-            spread = sb.tile([P, N], F32, name="cn_late%d" % g)
-            nc.sync.dma_start(out=spread[:], in_=cn[g, 0, :].partition_broadcast(P))
+        for h in range(2):
+            spread = sb.tile([P, 2, HALF], F32, name="cn_late%d" % h)
+            nc.sync.dma_start(out=spread[:], in_=cn[2:4, 0, h * HALF : (h + 1) * HALF].partition_broadcast(P))
             cn_late.append(spread)
 
         def interleave(copy, grouped, raw, k):
@@ -101,65 +101,43 @@ def tile_rows_kern_matern_kernel(tc, x, c, xn, cn, out):
         banks = [[ps.tile([P, N], F32, name="z%d_%d" % (g, b)) for b in range(2)] for g in range(G)]
         r = [[sb.tile([P, N], F32, name="r%d_%d" % (g, t)) for t in range(TILES)] for g in range(G)]
 
-        def product(z, g, t, h, k):
-            rows = slice(ROWS * g, ROWS * (g + 1))
-            m_cols = slice(t * P, (t + 1) * P)
-            n_cols = slice(k * CHUNK, (k + 1) * CHUNK)
-            nc.tensor.matmul_mx(
-                out=z,
-                lhsT=xq[1][rows, m_cols].bitcast(FP8X4),
-                lhsT_scale=xq[2][rows, m_cols],
-                rhs=cq[h][1][rows, n_cols].bitcast(FP8X4),
-                rhs_scale=cq[h][2][rows, n_cols],
-                start=True,
-                stop=True,
-            )
-
-        def products_by_half(g, h):
+        def products(pair, h):
             for k in range(2):
+                n_cols = slice(k * CHUNK, (k + 1) * CHUNK)
                 for t in range(TILES):
+                    m_cols = slice(t * P, (t + 1) * P)
                     c0 = t * HALF + k * CHUNK
-                    product(banks[g][h][:, c0 : c0 + CHUNK], g, t, h, k)
+                    for g in (2 * pair, 2 * pair + 1):
+                        rows = slice(ROWS * g, ROWS * (g + 1))
+                        nc.tensor.matmul_mx(
+                            out=banks[g][h][:, c0 : c0 + CHUNK],
+                            lhsT=xq[1][rows, m_cols].bitcast(FP8X4),
+                            lhsT_scale=xq[2][rows, m_cols],
+                            rhs=cq[h][1][rows, n_cols].bitcast(FP8X4),
+                            rhs_scale=cq[h][2][rows, n_cols],
+                            start=True,
+                            stop=True,
+                        )
 
-        def products_by_tile(g, t):
-            for h in range(2):
-                for k in range(2):
-                    c0 = h * HALF + k * CHUNK
-                    product(banks[g][t][:, c0 : c0 + CHUNK], g, t, h, k)
-
-        def root(g, t, n0, n1, part):
-            nc.scalar.activation(
-                out=r[g][t][:, n0:n1],
-                in_=part,
-                func=ACT.Sqrt,
-                bias=bias[:, TILES * g + t : TILES * g + t + 1],
-                scale=ROOT3_SQ,
-            )
-
-        def roots_by_half(g, h, t0, t1):
+        def roots(g, h, t0, t1):
             part = sb.tile([P, t1 - t0, HALF], F32, name="part%d_%d_%d" % (g, h, t0))
+            cn_row = (cn_early, cn_late)[g // 2][h][:, g % 2, :]
             nc.vector.scalar_tensor_tensor(
                 out=part[:],
                 in0=banks[g][h][:].rearrange("p (t n) -> p t n", t=TILES)[:, t0:t1, :],
                 scalar=-2.0,
-                in1=cn_early[h][:, g, :].unsqueeze(1).to_broadcast([P, t1 - t0, HALF]),
+                in1=cn_row.unsqueeze(1).to_broadcast([P, t1 - t0, HALF]),
                 op0=ALU.mult,
                 op1=ALU.add,
             )
             for t in range(t0, t1):
-                root(g, t, h * HALF, (h + 1) * HALF, part[:, t - t0, :])
-
-        def roots_by_tile(g, t, n0, n1):
-            part = sb.tile([P, n1 - n0], F32, name="part%d_%d_%d" % (g, t, n0))
-            nc.vector.scalar_tensor_tensor(
-                out=part[:],
-                in0=banks[g][t][:, n0:n1],
-                scalar=-2.0,
-                in1=cn_late[g - 2][:, n0:n1],
-                op0=ALU.mult,
-                op1=ALU.add,
-            )
-            root(g, t, n0, n1, part[:])
+                nc.scalar.activation(
+                    out=r[g][t][:, h * HALF : (h + 1) * HALF],
+                    in_=part[:, t - t0, :],
+                    func=ACT.Sqrt,
+                    bias=bias[:, TILES * g + t : TILES * g + t + 1],
+                    scale=ROOT3_SQ,
+                )
 
         wide = [repeat_cn(nc.vector.tensor_copy, 0), repeat_cn(nc.scalar.copy, 1)]
         cn_early = [spread_cn(wide[h], h) for h in range(2)]
@@ -171,27 +149,21 @@ def tile_rows_kern_matern_kernel(tc, x, c, xn, cn, out):
         quantize(xq, 0, 2)
         quantize(cq[0], 0, 1)
         quantize(cq[0], 1, 2)
-        for g in range(2):
-            products_by_half(g, 0)
+        products(0, 0)
         interleave(nc.vector.tensor_copy, cq[1][0], c_raw[1], 0)
         interleave(nc.scalar.copy, cq[1][0], c_raw[1], 1)
         nc.vector.tensor_scalar(out=bias[:], in0=xn_cols[:, 0:32:4], scalar1=ROOT3_SQ, scalar2=None, op0=ALU.mult)
         quantize(cq[1], 0, 2)
-        for g in range(2):
-            products_by_half(g, 1)
-        for g in range(2, G):
-            for t in range(TILES):
-                products_by_tile(g, t)
-        for t in range(TILES):
-            roots_by_half(0, 0, t, t + 1)
-        roots_by_half(1, 0, 0, TILES)
-        for g in range(2):
-            roots_by_half(g, 1, 0, TILES)
-        roots_by_tile(2, 0, 0, N)
-        roots_by_tile(2, 1, 0, N)
-        roots_by_tile(3, 0, 0, N)
-        roots_by_tile(3, 1, 0, HALF)
-        roots_by_tile(3, 1, HALF, N)
+        products(0, 1)
+        products(1, 0)
+        products(1, 1)
+        order = [(g, h) for pair in range(2) for h in range(2) for g in (2 * pair, 2 * pair + 1)]
+        for g, h in order:
+            if (g, h) in (order[0], order[-1]):
+                for t in range(TILES):
+                    roots(g, h, t, t + 1)
+            else:
+                roots(g, h, 0, TILES)
 
         for g in range(G):
             for t in range(TILES):

from contextlib import ExitStack

import concourse.mybir as mybir

G, D, M, N = 4, 128, 256, 512
FLOPS = 2 * G * D * M * N

F32 = mybir.dt.float32
BF16 = mybir.dt.bfloat16
U32 = mybir.dt.uint32
U8 = mybir.dt.uint8
FP8X4 = mybir.dt.float8_e4m3fn_x4
ALU = mybir.AluOpType
ACT = mybir.ActivationFunctionType

P = 128
PACK = 4
ROWS = D // PACK
CHUNK = 128
HALF = N // 2
TILES = M // P
ROOT3_SQ = 1.7320508 * 1.7320508


def tile_rows_kern_matern_kernel(tc, x, c, xn, cn, out):
    nc = tc.nc
    with ExitStack() as ctx:
        sb = ctx.enter_context(tc.tile_pool(name="sb", bufs=1))
        ps = ctx.enter_context(tc.psum_pool(name="ps", bufs=1))
        ctx.enter_context(tc.manual_schedule())

        x_rows = x.rearrange("g (p j) m -> (g p) j m", j=PACK)
        c_rows = c.rearrange("g (p j) n -> (g p) j n", j=PACK)

        ones = sb.tile([P, 1], F32, name="ones")
        nc.vector.memset(ones[:], 1.0)
        one = sb.tile([P, 1], F32, name="one")
        nc.scalar.activation(out=one[:], in_=ones[:], func=ACT.Sqrt)

        cn_rows = sb.tile([P, 32], F32, name="cn_rows", align_bytes=64)
        nc.sync.dma_start(
            out=cn_rows[:], in_=cn[0:2, 0, :].rearrange("g (b j) -> (g b) j", j=32).partition_broadcast(4)
        )
        x_raw = sb.tile([P, PACK, M], F32, name="x_raw")
        nc.sync.dma_start(out=x_raw[:], in_=x_rows)
        c_raw = [sb.tile([P, PACK, HALF], F32, name="c_raw%d" % h) for h in range(2)]
        nc.sync.dma_start(out=c_raw[0][:], in_=c_rows[:, :, 0:HALF])
        xn_rows = sb.tile([P, 32], F32, name="xn_rows", align_bytes=64)
        nc.vector.memset(xn_rows[:], 0.0)
        nc.sync.dma_start(out=xn_rows[0:P:4, :], in_=xn.rearrange("g (t q i) o -> q (g t) (i o)", q=4, i=32))
        nc.sync.dma_start(out=c_raw[1][:], in_=c_rows[:, :, HALF:N])
        cn_late = []
        for h in range(2):
            spread = sb.tile([P, 2, HALF], F32, name="cn_late%d" % h)
            nc.sync.dma_start(out=spread[:], in_=cn[2:4, 0, h * HALF : (h + 1) * HALF].partition_broadcast(P))
            cn_late.append(spread)

        def interleave(copy, grouped, raw, k):
            cols = slice(k * CHUNK, (k + 1) * CHUNK)
            copy(
                out=grouped[:, cols, :].rearrange("p (c i) j -> p c j i", i=4),
                in_=raw[:, :, cols].rearrange("p j (c i) -> p c j i", i=4),
            )

        def operand(name):
            grouped = sb.tile([P, 2 * CHUNK, PACK], BF16, name=name + "_grouped", align_bytes=64)
            codes = sb.tile([P, 2 * CHUNK], U32, name=name + "_codes", align_bytes=64)
            scales = sb.tile([P, 2 * CHUNK], U8, name=name + "_scales", align_bytes=64)
            return grouped, codes, scales

        def quantize(op, k0, k1):
            grouped, codes, scales = op
            cols = slice(k0 * CHUNK, k1 * CHUNK)
            nc.vector.quantize_mx(
                out=codes[:, cols].bitcast(FP8X4),
                scales=scales[:, cols],
                in_=grouped[:, cols, :].rearrange("p c j -> p (c j)"),
            )

        xq = operand("x")
        cq = [operand("c%d" % h) for h in range(2)]

        cn_cols = sb.tile([P, 32], F32, name="cn_cols", align_bytes=64)
        nc.vector.transpose(out=cn_cols[:], in_=cn_rows[:])
        xn_cols = sb.tile([P, 32], F32, name="xn_cols", align_bytes=64)
        bias = sb.tile([P, G * TILES], F32, name="bias")

        def repeat_cn(copy, h):
            wide = sb.tile([P, 2, 8, 32], F32, name="cn_wide%d" % h, align_bytes=64)
            blocks = cn_cols[:].rearrange("p (g h w) -> p g h w", g=2, h=2)[:, :, h, :]
            copy(out=wide[:], in_=blocks.unsqueeze(3).to_broadcast([P, 2, 8, 32]))
            return wide

        def spread_cn(wide, h):
            spread = sb.tile([P, 2, HALF], F32, name="cn_early%d" % h, align_bytes=64)
            nc.vector.transpose(
                out=spread[:].rearrange("p g n -> p (g n)"), in_=wide[:].rearrange("p g w i -> p (g w i)")
            )
            return spread

        banks = [[ps.tile([P, N], F32, name="z%d_%d" % (g, b)) for b in range(2)] for g in range(G)]
        r = [[sb.tile([P, N], F32, name="r%d_%d" % (g, t)) for t in range(TILES)] for g in range(G)]

        def products(pair, h):
            for k in range(2):
                n_cols = slice(k * CHUNK, (k + 1) * CHUNK)
                for t in range(TILES):
                    m_cols = slice(t * P, (t + 1) * P)
                    c0 = t * HALF + k * CHUNK
                    for g in (2 * pair, 2 * pair + 1):
                        rows = slice(ROWS * g, ROWS * (g + 1))
                        nc.tensor.matmul_mx(
                            out=banks[g][h][:, c0 : c0 + CHUNK],
                            lhsT=xq[1][rows, m_cols].bitcast(FP8X4),
                            lhsT_scale=xq[2][rows, m_cols],
                            rhs=cq[h][1][rows, n_cols].bitcast(FP8X4),
                            rhs_scale=cq[h][2][rows, n_cols],
                            start=True,
                            stop=True,
                        )

        def roots(g, h, t0, t1):
            part = sb.tile([P, t1 - t0, HALF], F32, name="part%d_%d_%d" % (g, h, t0))
            cn_row = (cn_early, cn_late)[g // 2][h][:, g % 2, :]
            nc.vector.scalar_tensor_tensor(
                out=part[:],
                in0=banks[g][h][:].rearrange("p (t n) -> p t n", t=TILES)[:, t0:t1, :],
                scalar=-2.0,
                in1=cn_row.unsqueeze(1).to_broadcast([P, t1 - t0, HALF]),
                op0=ALU.mult,
                op1=ALU.add,
            )
            for t in range(t0, t1):
                nc.scalar.activation(
                    out=r[g][t][:, h * HALF : (h + 1) * HALF],
                    in_=part[:, t - t0, :],
                    func=ACT.Sqrt,
                    bias=bias[:, TILES * g + t : TILES * g + t + 1],
                    scale=ROOT3_SQ,
                )

        wide = [repeat_cn(nc.vector.tensor_copy, 0), repeat_cn(nc.scalar.copy, 1)]
        cn_early = [spread_cn(wide[h], h) for h in range(2)]
        for t in range(TILES):
            interleave(nc.scalar.copy, xq[0], x_raw, t)
        interleave(nc.vector.tensor_copy, cq[0][0], c_raw[0], 0)
        interleave(nc.scalar.copy, cq[0][0], c_raw[0], 1)
        nc.vector.transpose(out=xn_cols[:], in_=xn_rows[:])
        quantize(xq, 0, 2)
        quantize(cq[0], 0, 1)
        quantize(cq[0], 1, 2)
        products(0, 0)
        interleave(nc.vector.tensor_copy, cq[1][0], c_raw[1], 0)
        interleave(nc.scalar.copy, cq[1][0], c_raw[1], 1)
        nc.vector.tensor_scalar(out=bias[:], in0=xn_cols[:, 0:32:4], scalar1=ROOT3_SQ, scalar2=None, op0=ALU.mult)
        quantize(cq[1], 0, 2)
        products(0, 1)
        products(1, 0)
        products(1, 1)
        order = [(g, h) for pair in range(2) for h in range(2) for g in (2 * pair, 2 * pair + 1)]
        for g, h in order:
            if (g, h) in (order[0], order[-1]):
                for t in range(TILES):
                    roots(g, h, t, t + 1)
            else:
                roots(g, h, 0, TILES)

        for g in range(G):
            for t in range(TILES):
                last = g == G - 1 and t == TILES - 1
                edge = last or (g == 0 and t == 0)
                cuts = (0, HALF, HALF + CHUNK, N) if last else (0, HALF, N)
                y = sb.tile([P, N], F32, name="y%d_%d" % (g, t))
                for n0, n1 in zip(cuts, cuts[1:]):
                    decay = sb.tile([P, n1 - n0], F32, name="decay%d_%d_%d" % (g, t, n0))
                    nc.scalar.activation(out=decay[:], in_=r[g][t][:, n0:n1], func=ACT.Exp, scale=-1.0)
                    nc.vector.scalar_tensor_tensor(
                        out=y[:, n0:n1], in0=r[g][t][:, n0:n1], scalar=one[:], in1=decay[:], op0=ALU.add, op1=ALU.mult
                    )
                    if edge:
                        nc.sync.dma_start(out=out[g, t * P : (t + 1) * P, n0:n1], in_=y[:, n0:n1])
                if not edge:
                    nc.sync.dma_start(out=out[g, t * P : (t + 1) * P, :], in_=y[:])
